import numpy as np
import ml_dtypes


def mxq(x, axis, fmt="e4m3"):
    dtype, down = {"e4m3": (ml_dtypes.float8_e4m3fn, 7), "e5m2": (ml_dtypes.float8_e5m2, 14)}[fmt]
    v = np.moveaxis(np.asarray(x, np.float32).astype(ml_dtypes.bfloat16).astype(np.float64), axis, -1)
    blocks = v.reshape(v.shape[:-1] + (-1, 32))
    amax = np.abs(blocks).max(-1, keepdims=True)
    byte = np.maximum(np.where(amax > 0, np.frexp(amax)[1] - 1 + 127, 0) - down, 1)
    scale = np.exp2(byte - 127.0)
    codes = (blocks / scale).astype(np.float32).astype(dtype).astype(np.float64)
    return np.moveaxis((codes * scale).reshape(v.shape), -1, axis)


WIDE = False


def mx_kscale(k):
    if not WIDE:
        return np.ones(k)
    levels = np.array([10, -10, 5, -5, 0])
    if k % 512:
        return np.exp2(np.random.permutation(np.resize(levels, k // 32))).repeat(32)
    a = np.empty((k // 512, 16))
    for p in range(k // 512):
        a[p, :8] = np.random.permutation(np.resize(levels, 8))
        for g in range(8):
            far = levels[np.abs(levels - a[p, g]) >= 10]
            a[p, g + 8] = far[np.random.randint(len(far))]
    return np.exp2(a.ravel()).repeat(32)


def f64(x):
    return np.asarray(x).astype(np.float64)


def striped(idx):
    return np.tile(idx.reshape(-1, 16).T, (8, 1)).astype(np.uint16)


def unstriped(offs):
    return offs[:16].T.reshape(-1).astype(np.int64)


def striped8(idx):
    return np.concatenate([x.reshape(-1, 16).T for x in idx]).astype(np.uint16)


def runs(offs, k):
    lists = np.stack([offs[16 * r : 16 * r + 16].T.reshape(-1) for r in range(8)]).astype(np.int64)
    return lists[np.arange(k) % 512 // 64]


def pack_weight(w):
    k, n = w.shape
    w = f64(np.asarray(w, np.float32).astype(ml_dtypes.bfloat16)).reshape(k // 32, 32, n)
    amax = np.abs(w).max(1)
    byte = np.clip(np.where(amax > 0, np.frexp(amax)[1] - 1 + 127 - 7, 1), 1, 254)
    scaled = (w * np.exp2(127.0 - byte)[:, None, :]).reshape(k, n).astype(np.float32)
    words = np.ascontiguousarray(scaled.reshape(k // 512, 128, 4, n).transpose(0, 1, 3, 2)).astype(ml_dtypes.float8_e4m3fn).view(np.uint8)
    return words, np.ascontiguousarray(byte.astype(np.uint8).reshape(k // 512, 16, n))


def unpack_weight(words, scales):
    g, p, n, _ = words.shape
    vals = np.ascontiguousarray(words).view(ml_dtypes.float8_e4m3fn).astype(np.float64) * np.repeat(np.exp2(scales.astype(np.float64) - 127.0), 8, axis=1)[..., None]
    return vals.transpose(0, 1, 3, 2).reshape(g * 512, n)


E2M1 = np.array([0.0, 0.5, 1.0, 1.5, 2.0, 3.0, 4.0, 6.0, -0.0, -0.5, -1.0, -1.5, -2.0, -3.0, -4.0, -6.0])


def pack_fp4(w):
    k, n = w.shape
    w = f64(np.asarray(w, np.float32).astype(ml_dtypes.bfloat16)).reshape(k // 32, 32, n)
    amax = np.abs(w).max(1)
    mant, ex = np.frexp(amax / 6.0)
    byte = np.clip(np.where(amax > 0, np.where(mant > 0.5, ex, ex - 1) + 127, 1), 1, 254)
    scaled = (w * np.exp2(127.0 - byte)[:, None, :]).reshape(k, n).astype(np.float32)
    c = np.ascontiguousarray(scaled.reshape(k // 512, 128, 4, n).transpose(0, 1, 3, 2)).astype(ml_dtypes.float4_e2m1fn).view(np.uint8) & 0xF
    words = (c[..., 0::2] | (c[..., 1::2] << 4)).reshape(k // 512, 128, 2 * n)
    return np.ascontiguousarray(words), np.ascontiguousarray(byte.astype(np.uint8).reshape(k // 512, 16, n))


def unpack_fp4(words, scales):
    g, _, n = scales.shape
    words = np.ascontiguousarray(words).reshape(g, 128, n, 2)
    nib = np.empty((g, 128, n, 4), np.uint8)
    nib[..., 0::2] = words & 0xF
    nib[..., 1::2] = words >> 4
    vals = E2M1[nib] * np.repeat(np.exp2(scales.astype(np.float64) - 127.0), 8, axis=1)[..., None]
    return vals.transpose(0, 1, 3, 2).reshape(g * 512, n)


def sigmoid(v):
    return 1.0 / (1.0 + np.exp(-np.maximum(v, -700.0)))

def planes(y):
    n, m = y.shape
    v = y.astype(np.float32).astype(ml_dtypes.bfloat16).astype(np.float64).reshape(n // 32, 32, m)
    top = np.abs(v).max(1)
    byte = np.clip(np.where(top > 0, np.frexp(top)[1] - 1 + 127 - 7, 1), 1, 254)
    codes = (v * np.exp2(127.0 - byte)[:, None, :]).reshape(n, m).astype(np.float32).astype(ml_dtypes.float8_e4m3fn).view(np.uint8)
    words = codes.reshape(n // 512, 128, 4, m).transpose(0, 1, 3, 2)
    return np.ascontiguousarray(words), np.ascontiguousarray(byte.astype(np.uint8).reshape(n // 512, 16, m))


K, T, S, N, G, H = 512, 1024, 256, 512, 2048, 512


def setup_inputs():
    n = np.random.standard_normal
    s = mx_kscale(K)[:, None]
    u = mx_kscale(K)
    packed_xT = pack_weight(n((K, T)) * s)
    packed_dT = pack_weight(n((K, G)) / s)
    packed_w1 = pack_fp4(n((H, N)) / np.sqrt(H) / u[:, None])
    return {
        "x_words": packed_xT[0],
        "x_scales": packed_xT[1],
        "d_words": packed_dT[0],
        "d_scales": packed_dT[1],
        "tau": np.random.uniform(0.3, 0.9, (H, 1)).astype(np.float32),
        "gn": (np.random.uniform(0.5, 1.5, (H, 1)) * u[:, None]).astype(np.float32),
        "w1_words": packed_w1[0],
        "w1_scales": packed_w1[1],
        "sl": np.random.uniform(1.5, 2.5, (N, 1)).astype(np.float32),
        "lo": np.random.uniform(-1.2, -0.4, (N, 1)).astype(np.float32),
        "hi": np.random.uniform(0.4, 1.2, (N, 1)).astype(np.float32),
        "offs": striped(np.random.permutation(T)[:S]),
        "k1": striped8(np.random.randint(0, G, (8, H))),
        "two": striped(np.random.permutation(T)[:S]),
        "k2": striped8(np.random.randint(0, G, (8, H))),
        "n1": striped(np.random.permutation(S)),
        "n2": striped(np.random.permutation(S)),
        "n3": striped8(np.stack([np.random.permutation(S) for _ in range(8)])),
    }


def reference(x_words, x_scales, d_words, d_scales, tau, gn, w1_words, w1_scales, sl, lo, hi, offs, k1, two, k2, n1, n2, n3):
    d_k1 = unpack_weight(d_words, d_scales)[np.arange(K)[:, None], runs(k1, K)]
    xq = unpack_weight(x_words, x_scales)[:, unstriped(offs)]
    a = 0.0625 * (d_k1.T @ xq)
    d_k2 = unpack_weight(d_words, d_scales)[np.arange(K)[:, None], runs(k2, K)]
    x_two = unpack_weight(x_words, x_scales)[:, unstriped(two)]
    b = 0.0625 * (d_k2.T @ x_two)
    top = b.max(axis=1, keepdims=True)
    ea = np.exp(f64(tau) * (b[:, unstriped(n1)] - top))
    z = f64(gn) * ((0.5 * (a - a[:, unstriped(n2)])) / (ea + 0.25))
    h = unpack_fp4(w1_words, w1_scales).T @ mxq(z, 0, "e4m3")
    sg = sigmoid(f64(sl) * (h[np.arange(N)[:, None], runs(n3, N)] - f64(lo)))
    sg2 = sigmoid(f64(sl) * (h[np.arange(N)[:, None], runs(n3, N)] - f64(hi)))
    out_0 = h * (sg - sg2)
    return (out_0,) + planes(out_0)

@@ -1,0 +1,230 @@
+from contextlib import ExitStack
+
+import concourse.mybir as mybir
+
+K, T, S, N, G, H = 512, 1024, 256, 512, 2048, 512
+FLOPS = 2 * K * H * S * 2 + 2 * H * N * S
+
+F32 = mybir.dt.float32
+BF16 = mybir.dt.bfloat16
+I32 = mybir.dt.int32
+U32 = mybir.dt.uint32
+U16 = mybir.dt.uint16
+U8 = mybir.dt.uint8
+FP8X4 = mybir.dt.float8_e4m3fn_x4
+FP4X4 = mybir.dt.float4_e2m1fn_x4
+ALU = mybir.AluOpType
+ACT = mybir.ActivationFunctionType
+
+P = 128
+PACK = 4
+HALF = S // 2
+LOWEST = -3.0e38
+
+
+def tile_picked_twpqqxbebd_none_po_kernel(
+    tc, x_words, x_scales, d_words, d_scales, tau, gn, w1_words, w1_scales, sl, lo, hi,
+    offs, k1, two, k2, n1, n2, n3, out_0, out_1, out_2,
+):
+    nc = tc.nc
+    with ExitStack() as ctx:
+        sb = ctx.enter_context(tc.tile_pool(name="sb", bufs=1))
+        ps = ctx.enter_context(tc.psum_pool(name="ps", bufs=1))
+
+        def tile(name, shape, dtype, tag=""):
+            return sb.tile(shape, dtype, name=name, tag=tag or name, align_bytes=64)
+
+        def load_list(name, src):
+            dst = sb.tile([P, src.shape[1]], U16, name=name)
+            nc.sync.dma_start(dst[:], src)
+            return dst
+
+        def load_column(queue, name, src):
+            dst = tile(name, [P, PACK], F32)
+            queue.dma_start(dst[:], src.rearrange("(p t) o -> p (t o)", t=PACK))
+            return dst
+
+        def half_of(lst, u):
+            return lst[:, u * (HALF // 16) : (u + 1) * (HALF // 16)]
+
+        d_sc = tile("d_sc", [P, G], U8)
+        x_sc = tile("x_sc", [P, T], U8)
+        k2_t = load_list("k2_t", k2)
+        nc.sync.dma_start(d_sc[:].bitcast(I32), d_scales[0].bitcast(I32).unsqueeze(1).to_broadcast([16, 8, G // 4]))
+        two_t = load_list("two_t", two)
+        nc.sync.dma_start(x_sc[:].bitcast(I32), x_scales[0].bitcast(I32).unsqueeze(1).to_broadcast([16, 8, T // 4]))
+        d_w = tile("d_w", [P, G], U32)
+        x_w = tile("x_w", [P, T], U32)
+        nc.sync.dma_start(d_w[:].bitcast(I32), d_words[0].rearrange("p c r -> p (c r)").bitcast(I32))
+        k1_t = load_list("k1_t", k1)
+        offs_t = load_list("offs_t", offs)
+        nc.sync.dma_start(x_w[:].bitcast(I32), x_words[0].rearrange("p c r -> p (c r)").bitcast(I32))
+        n1_t = load_list("n1_t", n1)
+        n2_t = load_list("n2_t", n2)
+        n3_t = load_list("n3_t", n3)
+        tau_t = load_column(nc.gpsimd, "tau_t", tau)
+
+        moved = {}
+        for name in ("b", "a"):
+            moved[name] = tile("moved_" + name, [P, H + S], U8)
+            nc.vector.memset(moved[name][:].bitcast(I32), 0)
+        out_sc = tile("out_sc", [P, S], U8)
+        z_sc = tile("z_sc", [P, S], U8)
+
+        w_sc_raw = tile("w_sc_raw", [P, N], U8)
+        nc.vector.memset(w_sc_raw[:].bitcast(I32), 0)
+        for q in range(4):
+            nc.gpsimd.dma_start(
+                w_sc_raw[:].bitcast(I32)[32 * q : 32 * q + 4, :], w1_scales[0].bitcast(I32)[4 * q : 4 * q + 4, :]
+            )
+        gn_t = load_column(nc.gpsimd, "gn_t", gn)
+        w_raw = tile("w_raw", [P, 2 * N], U8)
+        nc.gpsimd.dma_start(w_raw[:].bitcast(I32), w1_words[0].bitcast(I32))
+        sl_t = load_column(nc.gpsimd, "sl_t", sl)
+        lo_t = load_column(nc.gpsimd, "lo_t", lo)
+        hi_t = load_column(nc.gpsimd, "hi_t", hi)
+
+        neg_tau = tile("neg_tau", [P, PACK], F32)
+        nc.scalar.activation(neg_tau[:], tau_t[:], ACT.Copy, scale=-1.0)
+
+        def coded_product(name, k_t, x_t, slots):
+            picked_sc = tile("picked_sc_" + name, [P, H + S], U8, slots[0])
+            nc.vector.tensor_copy(picked_sc[:, 0:H], d_sc[:].indirect(k_t[:]))
+            nc.vector.tensor_copy(picked_sc[:, H : H + S], x_sc[:].indirect(x_t[:]))
+            for q in range(4):
+                nc.sync.dma_start(
+                    moved[name][:].bitcast(I32)[32 * q : 32 * q + 4, :],
+                    picked_sc[:].bitcast(I32)[32 * q : 32 * q + 32 : 8, :],
+                )
+            picked_d = tile("picked_d_" + name, [P, H], U32, slots[1])
+            nc.vector.tensor_copy(picked_d[:], d_w[:].indirect(k_t[:]))
+            dealt_d = tile("dealt_d_" + name, [P, H], U32, slots[2])
+            nc.vector.tensor_copy(
+                dealt_d[:].bitcast(I32).rearrange("p (t m) -> p m t", t=PACK),
+                picked_d[:].bitcast(I32).rearrange("p (m t) -> p m t", t=PACK),
+            )
+            picked_x = tile("picked_x_" + name, [P, S], U32, slots[3])
+            nc.vector.tensor_copy(picked_x[:], x_w[:].indirect(x_t[:]))
+            dealt_sc = tile("dealt_sc_" + name, [P, H], U8, slots[4])
+            nc.vector.tensor_copy(
+                dealt_sc[:].rearrange("p (t m) -> p m t", t=PACK),
+                moved[name][:, 0:H].rearrange("p (m t) -> p m t", t=PACK),
+            )
+            banks = []
+            for t in range(PACK):
+                bank = ps.tile([P, S], F32, name="bank_%s%d" % (name, t), tag="bank_%s%d" % (name, t))
+                nc.tensor.matmul_mx(
+                    bank[:],
+                    lhsT=dealt_d[:, t * P : (t + 1) * P].bitcast(FP8X4),
+                    lhsT_scale=dealt_sc[:, t * P : (t + 1) * P],
+                    rhs=picked_x[:].bitcast(FP8X4),
+                    rhs_scale=moved[name][:, H : H + S],
+                    start=True,
+                    stop=True,
+                )
+                banks.append(bank)
+            return banks
+
+        b_banks = coded_product("b", k2_t, two_t, ("s0", "s1", "s2", "s3", "s4"))
+        w_sc = tile("w_sc", [P, N], U8, "s0")
+        ea = tile("ea", [P, PACK, S], F32)
+        for t in range(PACK):
+            b_row = tile("b_row%d" % t, [P, S], F32)
+            top = tile("top%d" % t, [P, 1], F32)
+            nc.vector.tensor_scalar(b_row[:], b_banks[t][:], 0.0625, LOWEST, ALU.mult, ALU.max, accum_out=top[:])
+            exp_bias = tile("exp_bias%d" % t, [P, 1], F32)
+            nc.scalar.activation(exp_bias[:], top[:], ACT.Copy, scale=neg_tau[:, t : t + 1])
+            for u in range(2):
+                nc.scalar.activation(
+                    ea[:, t, u * HALF : (u + 1) * HALF], b_row[:].indirect(half_of(n1_t, u)), ACT.Exp,
+                    bias=exp_bias[:], scale=tau_t[:, t : t + 1],
+                )
+
+        a_banks = coded_product("a", k1_t, offs_t, ("s3", "s2", "s1", "s4", "s5"))
+
+        root = tile("root", [P, PACK * S], F32)
+        nc.scalar.activation(root[:], ea[:].rearrange("p t n -> p (t n)"), ACT.Abs_reciprocal_sqrt, bias=0.25)
+        inv = tile("inv", [P, PACK, S], F32)
+        nc.scalar.activation(inv[:].rearrange("p t n -> p (t n)"), root[:], ACT.Square)
+
+        w_dealt = tile("w_dealt", [P, 2 * N], U8)
+        nc.scalar.copy(
+            w_dealt[:].bitcast(U16).rearrange("p (t m) -> p m t", t=PACK),
+            w_raw[:].bitcast(U16).rearrange("p (m t) -> p m t", t=PACK),
+        )
+        nc.vector.tensor_copy(
+            w_sc[:].rearrange("p (t m) -> p m t", t=PACK), w_sc_raw[:].rearrange("p (m t) -> p m t", t=PACK)
+        )
+        neg_sl = tile("neg_sl", [P, PACK], F32)
+        nc.gpsimd.tensor_scalar(neg_sl[:], sl_t[:], -1.0, 0.0, ALU.mult, ALU.add)
+        bias_lo = tile("bias_lo", [P, PACK], F32)
+        nc.gpsimd.tensor_tensor(bias_lo[:], neg_sl[:], lo_t[:], ALU.mult)
+        bias_hi = tile("bias_hi", [P, PACK], F32)
+        nc.gpsimd.tensor_tensor(bias_hi[:], neg_sl[:], hi_t[:], ALU.mult)
+
+        a_rows = tile("a_rows", [P, PACK, S], F32)
+        for t in range(PACK):
+            nc.vector.tensor_scalar(a_rows[:, t, :], a_banks[t][:], gn_t[:, t : t + 1], 0.03125, ALU.mult, ALU.mult)
+
+        z_codes = tile("z_codes", [P, S], U32)
+        h_banks = [ps.tile([P, S], F32, name="bank_h%d" % t, tag="bank_b%d" % t) for t in range(PACK)]
+        for u in range(2):
+            cols = slice(u * HALF, (u + 1) * HALF)
+            a_far = tile("a_far%d" % u, [P, PACK, HALF], F32)
+            for t in range(PACK):
+                nc.scalar.activation(a_far[:, t, :], a_rows[:, t, :].indirect(half_of(n2_t, u)), ACT.Copy)
+            diff = tile("diff%d" % u, [P, PACK, HALF], F32)
+            nc.vector.tensor_tensor(diff[:], a_rows[:, :, cols], a_far[:], ALU.subtract)
+            z_bf = tile("z_bf%d" % u, [P, PACK * HALF], BF16)
+            nc.vector.tensor_tensor(
+                z_bf[:].rearrange("p (c i t) -> p c t i", i=4, t=PACK),
+                diff[:].rearrange("p t (c i) -> p c t i", i=4),
+                inv[:, :, cols].rearrange("p t (c i) -> p c t i", i=4),
+                ALU.mult,
+            )
+            nc.vector.quantize_mx(z_codes[:, cols].bitcast(FP8X4), z_sc[:, cols], z_bf[:])
+            for t in range(PACK):
+                nc.tensor.matmul_mx(
+                    h_banks[t][:, cols],
+                    lhsT=w_dealt[:, 2 * t * P : 2 * (t + 1) * P].bitcast(FP4X4),
+                    lhsT_scale=w_sc[:, t * P : (t + 1) * P],
+                    rhs=z_codes[:, cols].bitcast(FP8X4),
+                    rhs_scale=z_sc[:, cols],
+                    start=True,
+                    stop=True,
+                )
+
+        h_rows = []
+        for t in range(PACK):
+            h_row = tile("h_row%d" % t, [P, S], F32)
+            nc.vector.tensor_copy(h_row[:], h_banks[t][:])
+            h_rows.append(h_row)
+
+        out_codes = tile("out_codes", [P, S], U32)
+        out_rows = out_0.rearrange("(p t) n -> p t n", t=PACK)
+        codes_dram = out_1[0].rearrange("p c r -> p (c r)").bitcast(I32)
+        for u in range(2):
+            cols = slice(u * HALF, (u + 1) * HALF)
+            y = tile("y%d" % u, [P, PACK, HALF], F32)
+            for t in range(PACK):
+                sg = tile("sg%d%d" % (u, t), [P, HALF], F32)
+                sg2 = tile("sg2%d%d" % (u, t), [P, HALF], F32)
+                for dst, bias in ((sg, bias_lo), (sg2, bias_hi)):
+                    nc.scalar.activation(
+                        dst[:], h_rows[t][:].indirect(half_of(n3_t, u)), ACT.Sigmoid,
+                        bias=bias[:, t : t + 1], scale=sl_t[:, t : t + 1],
+                    )
+                band = tile("band%d%d" % (u, t), [P, HALF], F32)
+                nc.vector.tensor_tensor(band[:], sg[:], sg2[:], ALU.subtract)
+                nc.vector.tensor_tensor(y[:, t, :], h_rows[t][:, cols], band[:], ALU.mult)
+            nc.sync.dma_start(out_rows[:, :, cols], y[:])
+            y_bf = tile("y_bf%d" % u, [P, PACK * HALF], BF16)
+            nc.vector.tensor_copy(
+                y_bf[:].rearrange("p (c i t) -> p c t i", i=4, t=PACK),
+                y[:].rearrange("p t (c i) -> p c t i", i=4),
+            )
+            nc.vector.quantize_mx(out_codes[:, cols].bitcast(FP8X4), out_sc[:, cols], y_bf[:])
+            nc.sync.dma_start(codes_dram[:, cols], out_codes[:, cols].bitcast(I32))
+        for q in range(4):
+            queue = nc.scalar if q % 2 == 0 else nc.sync
+            queue.dma_start(out_2[0].bitcast(I32)[4 * q : 4 * q + 4, :], out_sc[:].bitcast(I32)[32 * q : 32 * q + 4, :])

@@ -19,6 +19,7 @@ ACT = mybir.ActivationFunctionType
 P = 128
 PACK = 4
 HALF = S // 2
+QUARTER = S // 4
 LOWEST = -3.0e38
 
 
@@ -49,25 +50,28 @@ def tile_picked_twpqqxbebd_none_po_kernel(
 
         d_sc = tile("d_sc", [P, G], U8)
         x_sc = tile("x_sc", [P, T], U8)
-        k2_t = load_list("k2_t", k2)
-        nc.sync.dma_start(d_sc[:].bitcast(I32), d_scales[0].bitcast(I32).unsqueeze(1).to_broadcast([16, 8, G // 4]))
         two_t = load_list("two_t", two)
         nc.sync.dma_start(x_sc[:].bitcast(I32), x_scales[0].bitcast(I32).unsqueeze(1).to_broadcast([16, 8, T // 4]))
+        k2_t = load_list("k2_t", k2)
+        nc.sync.dma_start(d_sc[:].bitcast(I32), d_scales[0].bitcast(I32).unsqueeze(1).to_broadcast([16, 8, G // 4]))
         d_w = tile("d_w", [P, G], U32)
         x_w = tile("x_w", [P, T], U32)
-        nc.sync.dma_start(d_w[:].bitcast(I32), d_words[0].rearrange("p c r -> p (c r)").bitcast(I32))
-        k1_t = load_list("k1_t", k1)
         offs_t = load_list("offs_t", offs)
-        nc.sync.dma_start(x_w[:].bitcast(I32), x_words[0].rearrange("p c r -> p (c r)").bitcast(I32))
+        k1_t = load_list("k1_t", k1)
         n1_t = load_list("n1_t", n1)
+        nc.sync.dma_start(d_w[:].bitcast(I32), d_words[0].rearrange("p c r -> p (c r)").bitcast(I32))
         n2_t = load_list("n2_t", n2)
         n3_t = load_list("n3_t", n3)
+        nc.sync.dma_start(x_w[:].bitcast(I32), x_words[0].rearrange("p c r -> p (c r)").bitcast(I32))
         tau_t = load_column(nc.gpsimd, "tau_t", tau)
 
         moved = {}
-        for name in ("b", "a"):
-            moved[name] = tile("moved_" + name, [P, H + S], U8)
+        for name, width in (("b", H + S), ("ax", S), ("a", H)):
+            moved[name] = tile("moved_" + name, [P, width], U8)
             nc.vector.memset(moved[name][:].bitcast(I32), 0)
+        b_rows = [tile("b_row%d" % t, [P, 2 * S], F32) for t in range(PACK)]
+        for b_row in b_rows:
+            nc.vector.memset(b_row[:, S : 2 * S], 0.0)
         out_sc = tile("out_sc", [P, S], U8)
         z_sc = tile("z_sc", [P, S], U8)
 
@@ -87,15 +91,14 @@ def tile_picked_twpqqxbebd_none_po_kernel(
         neg_tau = tile("neg_tau", [P, PACK], F32)
         nc.scalar.activation(neg_tau[:], tau_t[:], ACT.Copy, scale=-1.0)
 
-        def coded_product(name, k_t, x_t, slots):
-            picked_sc = tile("picked_sc_" + name, [P, H + S], U8, slots[0])
-            nc.vector.tensor_copy(picked_sc[:, 0:H], d_sc[:].indirect(k_t[:]))
-            nc.vector.tensor_copy(picked_sc[:, H : H + S], x_sc[:].indirect(x_t[:]))
+        def move_rows(name, picked_sc):
             for q in range(4):
                 nc.sync.dma_start(
                     moved[name][:].bitcast(I32)[32 * q : 32 * q + 4, :],
                     picked_sc[:].bitcast(I32)[32 * q : 32 * q + 32 : 8, :],
                 )
+
+        def coded_product(name, k_t, x_t, x_plane, slots):
             picked_d = tile("picked_d_" + name, [P, H], U32, slots[1])
             nc.vector.tensor_copy(picked_d[:], d_w[:].indirect(k_t[:]))
             dealt_d = tile("dealt_d_" + name, [P, H], U32, slots[2])
@@ -118,29 +121,37 @@ def tile_picked_twpqqxbebd_none_po_kernel(
                     lhsT=dealt_d[:, t * P : (t + 1) * P].bitcast(FP8X4),
                     lhsT_scale=dealt_sc[:, t * P : (t + 1) * P],
                     rhs=picked_x[:].bitcast(FP8X4),
-                    rhs_scale=moved[name][:, H : H + S],
+                    rhs_scale=x_plane,
                     start=True,
                     stop=True,
                 )
                 banks.append(bank)
             return banks
 
-        b_banks = coded_product("b", k2_t, two_t, ("s0", "s1", "s2", "s3", "s4"))
-        w_sc = tile("w_sc", [P, N], U8, "s0")
+        picked_sc_b = tile("picked_sc_b", [P, H + S], U8, "s0")
+        nc.vector.tensor_copy(picked_sc_b[:, H : H + S], x_sc[:].indirect(two_t[:]))
+        nc.vector.tensor_copy(picked_sc_b[:, 0:H], d_sc[:].indirect(k2_t[:]))
+        move_rows("b", picked_sc_b)
+        picked_sc_ax = tile("picked_sc_ax", [P, S], U8)
+        nc.vector.tensor_copy(picked_sc_ax[:], x_sc[:].indirect(offs_t[:]))
+        move_rows("ax", picked_sc_ax)
+        b_banks = coded_product("b", k2_t, two_t, moved["b"][:, H : H + S], ("s0", "s1", "s2", "s3", "s4"))
+        picked_sc_a = tile("picked_sc_a", [P, H], U8, "s0")
+        nc.vector.tensor_copy(picked_sc_a[:], d_sc[:].indirect(k1_t[:]))
+        move_rows("a", picked_sc_a)
         ea = tile("ea", [P, PACK, S], F32)
         for t in range(PACK):
-            b_row = tile("b_row%d" % t, [P, S], F32)
+            b_row = b_rows[t]
             top = tile("top%d" % t, [P, 1], F32)
-            nc.vector.tensor_scalar(b_row[:], b_banks[t][:], 0.0625, LOWEST, ALU.mult, ALU.max, accum_out=top[:])
+            nc.vector.tensor_scalar(b_row[:, 0:S], b_banks[t][:], 0.0625, LOWEST, ALU.mult, ALU.max, accum_out=top[:])
             exp_bias = tile("exp_bias%d" % t, [P, 1], F32)
             nc.scalar.activation(exp_bias[:], top[:], ACT.Copy, scale=neg_tau[:, t : t + 1])
-            for u in range(2):
-                nc.scalar.activation(
-                    ea[:, t, u * HALF : (u + 1) * HALF], b_row[:].indirect(half_of(n1_t, u)), ACT.Exp,
-                    bias=exp_bias[:], scale=tau_t[:, t : t + 1],
-                )
+            nc.scalar.activation(
+                ea[:, t, :], b_row[:].indirect(n1_t[:]), ACT.Exp, bias=exp_bias[:], scale=tau_t[:, t : t + 1]
+            )
 
-        a_banks = coded_product("a", k1_t, offs_t, ("s3", "s2", "s1", "s4", "s5"))
+        a_banks = coded_product("a", k1_t, offs_t, moved["ax"][:], ("s0", "top0", "s1", "top1", "s5"))
+        w_sc = tile("w_sc", [P, N], U8, "s0")
 
         root = tile("root", [P, PACK * S], F32)
         nc.scalar.activation(root[:], ea[:].rearrange("p t n -> p (t n)"), ACT.Abs_reciprocal_sqrt, bias=0.25)
@@ -167,25 +178,38 @@ def tile_picked_twpqqxbebd_none_po_kernel(
             nc.vector.tensor_scalar(a_rows[:, t, :], a_banks[t][:], gn_t[:, t : t + 1], 0.03125, ALU.mult, ALU.mult)
 
         z_codes = tile("z_codes", [P, S], U32)
-        h_banks = [ps.tile([P, S], F32, name="bank_h%d" % t, tag="bank_b%d" % t) for t in range(PACK)]
+        h_rows = [tile("h_row%d" % t, [P, S], F32) for t in range(PACK)]
         for u in range(2):
             cols = slice(u * HALF, (u + 1) * HALF)
-            a_far = tile("a_far%d" % u, [P, PACK, HALF], F32)
+            a_far = tile("a_far%d" % u, [P, PACK, HALF], F32, "root" if u else "")
             for t in range(PACK):
-                nc.scalar.activation(a_far[:, t, :], a_rows[:, t, :].indirect(half_of(n2_t, u)), ACT.Copy)
-            diff = tile("diff%d" % u, [P, PACK, HALF], F32)
-            nc.vector.tensor_tensor(diff[:], a_rows[:, :, cols], a_far[:], ALU.subtract)
+                looked_up = a_rows[:, t, :].indirect(half_of(n2_t, u))
+                if u == 0:
+                    nc.vector.tensor_copy(a_far[:, t, :], looked_up)
+                else:
+                    nc.scalar.activation(a_far[:, t, :], looked_up, ACT.Copy)
+            diff = tile("diff%d" % u, [P, PACK, HALF], F32, "z_bf0" if u else "")
             z_bf = tile("z_bf%d" % u, [P, PACK * HALF], BF16)
-            nc.vector.tensor_tensor(
-                z_bf[:].rearrange("p (c i t) -> p c t i", i=4, t=PACK),
-                diff[:].rearrange("p t (c i) -> p c t i", i=4),
-                inv[:, :, cols].rearrange("p t (c i) -> p c t i", i=4),
-                ALU.mult,
-            )
-            nc.vector.quantize_mx(z_codes[:, cols].bitcast(FP8X4), z_sc[:, cols], z_bf[:])
+            parts = [slice(v * QUARTER, (v + 1) * QUARTER) for v in range(2)]
+            for part in parts:
+                nc.vector.tensor_tensor(diff[:, :, part], a_rows[:, :, cols][:, :, part], a_far[:, :, part], ALU.subtract)
+            for part in parts:
+                nc.vector.tensor_tensor(
+                    z_bf[:].rearrange("p (n t) -> p t n", t=PACK)[:, :, part].rearrange("p t (c i) -> p c t i", i=4),
+                    diff[:, :, part].rearrange("p t (c i) -> p c t i", i=4),
+                    inv[:, :, cols][:, :, part].rearrange("p t (c i) -> p c t i", i=4),
+                    ALU.mult,
+                )
+            for part in parts:
+                nc.vector.quantize_mx(
+                    z_codes[:, cols][:, part].bitcast(FP8X4),
+                    z_sc[:, cols][:, part],
+                    z_bf[:, PACK * part.start : PACK * part.stop],
+                )
             for t in range(PACK):
+                h_bank = ps.tile([P, HALF], F32, name="bank_h%d%d" % (u, t), tag="bank_%s%d" % ("ba"[u], t))
                 nc.tensor.matmul_mx(
-                    h_banks[t][:, cols],
+                    h_bank[:],
                     lhsT=w_dealt[:, 2 * t * P : 2 * (t + 1) * P].bitcast(FP4X4),
                     lhsT_scale=w_sc[:, t * P : (t + 1) * P],
                     rhs=z_codes[:, cols].bitcast(FP8X4),
@@ -193,12 +217,10 @@ def tile_picked_twpqqxbebd_none_po_kernel(
                     start=True,
                     stop=True,
                 )
-
-        h_rows = []
-        for t in range(PACK):
-            h_row = tile("h_row%d" % t, [P, S], F32)
-            nc.vector.tensor_copy(h_row[:], h_banks[t][:])
-            h_rows.append(h_row)
+                if u == 0:
+                    nc.scalar.copy(h_rows[t][:, cols], h_bank[:])
+                else:
+                    nc.vector.tensor_copy(h_rows[t][:, cols], h_bank[:])
 
         out_codes = tile("out_codes", [P, S], U32)
         out_rows = out_0.rearrange("(p t) n -> p t n", t=PACK)
@@ -206,6 +228,7 @@ def tile_picked_twpqqxbebd_none_po_kernel(
         for u in range(2):
             cols = slice(u * HALF, (u + 1) * HALF)
             y = tile("y%d" % u, [P, PACK, HALF], F32)
+            y_bf = tile("y_bf%d" % u, [P, PACK * HALF], BF16)
             for t in range(PACK):
                 sg = tile("sg%d%d" % (u, t), [P, HALF], F32)
                 sg2 = tile("sg2%d%d" % (u, t), [P, HALF], F32)
@@ -217,12 +240,13 @@ def tile_picked_twpqqxbebd_none_po_kernel(
                 band = tile("band%d%d" % (u, t), [P, HALF], F32)
                 nc.vector.tensor_tensor(band[:], sg[:], sg2[:], ALU.subtract)
                 nc.vector.tensor_tensor(y[:, t, :], h_rows[t][:, cols], band[:], ALU.mult)
-            nc.sync.dma_start(out_rows[:, :, cols], y[:])
-            y_bf = tile("y_bf%d" % u, [P, PACK * HALF], BF16)
-            nc.vector.tensor_copy(
-                y_bf[:].rearrange("p (c i t) -> p c t i", i=4, t=PACK),
-                y[:].rearrange("p t (c i) -> p c t i", i=4),
-            )
+                if t >= PACK - 2:
+                    rows = slice(0, PACK - 1) if t == PACK - 2 else slice(PACK - 1, PACK)
+                    nc.sync.dma_start(out_rows[:, rows, cols], y[:, rows, :])
+                    nc.vector.tensor_copy(
+                        y_bf[:].rearrange("p (c i t) -> p c t i", i=4, t=PACK)[:, :, rows, :],
+                        y[:, rows, :].rearrange("p t (c i) -> p c t i", i=4),
+                    )
             nc.vector.quantize_mx(out_codes[:, cols].bitcast(FP8X4), out_sc[:, cols], y_bf[:])
             nc.sync.dma_start(codes_dram[:, cols], out_codes[:, cols].bitcast(I32))
         for q in range(4):

@@ -75,18 +75,8 @@ def tile_picked_twpqqxbebd_none_po_kernel(
         out_sc = tile("out_sc", [P, S], U8)
         z_sc = tile("z_sc", [P, S], U8)
 
-        w_sc_raw = tile("w_sc_raw", [P, N], U8)
-        nc.vector.memset(w_sc_raw[:].bitcast(I32), 0)
-        for q in range(4):
-            nc.gpsimd.dma_start(
-                w_sc_raw[:].bitcast(I32)[32 * q : 32 * q + 4, :], w1_scales[0].bitcast(I32)[4 * q : 4 * q + 4, :]
-            )
-        gn_t = load_column(nc.gpsimd, "gn_t", gn)
         w_raw = tile("w_raw", [P, 2 * N], U8)
         nc.gpsimd.dma_start(w_raw[:].bitcast(I32), w1_words[0].bitcast(I32))
-        sl_t = load_column(nc.gpsimd, "sl_t", sl)
-        lo_t = load_column(nc.gpsimd, "lo_t", lo)
-        hi_t = load_column(nc.gpsimd, "hi_t", hi)
 
         neg_tau = tile("neg_tau", [P, PACK], F32)
         nc.scalar.activation(neg_tau[:], tau_t[:], ACT.Copy, scale=-1.0)
@@ -136,6 +126,16 @@ def tile_picked_twpqqxbebd_none_po_kernel(
         nc.vector.tensor_copy(picked_sc_ax[:], x_sc[:].indirect(offs_t[:]))
         move_rows("ax", picked_sc_ax)
         b_banks = coded_product("b", k2_t, two_t, moved["b"][:, H : H + S], ("s0", "s1", "s2", "s3", "s4"))
+        w_sc_raw = tile("w_sc_raw", [P, N], U8, "s1")
+        for q in range(4):
+            rows = w1_scales[0].bitcast(I32)[4 * q : 4 * q + 4, :]
+            nc.sync.dma_start(
+                w_sc_raw[:].bitcast(I32)[32 * q : 32 * q + 32, :], rows.unsqueeze(0).to_broadcast([8, 4, N // 4])
+            )
+        late = tile("late", [P, 4, 2 * PACK], F32, "picked_sc_ax")
+        for j, src in enumerate((gn, sl, lo, hi)):
+            nc.sync.dma_start(late[:, j, 0:PACK], src.rearrange("(p t) o -> p (t o)", t=PACK))
+        gn_t, sl_t, lo_t, hi_t = (late[:, j, 0:PACK] for j in range(4))
         picked_sc_a = tile("picked_sc_a", [P, H], U8, "s0")
         nc.vector.tensor_copy(picked_sc_a[:], d_sc[:].indirect(k1_t[:]))
         move_rows("a", picked_sc_a)
@@ -150,7 +150,7 @@ def tile_picked_twpqqxbebd_none_po_kernel(
                 ea[:, t, :], b_row[:].indirect(n1_t[:]), ACT.Exp, bias=exp_bias[:], scale=tau_t[:, t : t + 1]
             )
 
-        a_banks = coded_product("a", k1_t, offs_t, moved["ax"][:], ("s0", "top0", "s1", "top1", "s5"))
+        a_banks = coded_product("a", k1_t, offs_t, moved["ax"][:], ("s0", "top0", "s6", "top1", "s5"))
         w_sc = tile("w_sc", [P, N], U8, "s0")
 
         root = tile("root", [P, PACK * S], F32)
@@ -166,12 +166,10 @@ def tile_picked_twpqqxbebd_none_po_kernel(
         nc.vector.tensor_copy(
             w_sc[:].rearrange("p (t m) -> p m t", t=PACK), w_sc_raw[:].rearrange("p (m t) -> p m t", t=PACK)
         )
-        neg_sl = tile("neg_sl", [P, PACK], F32)
-        nc.gpsimd.tensor_scalar(neg_sl[:], sl_t[:], -1.0, 0.0, ALU.mult, ALU.add)
         bias_lo = tile("bias_lo", [P, PACK], F32)
-        nc.gpsimd.tensor_tensor(bias_lo[:], neg_sl[:], lo_t[:], ALU.mult)
+        nc.vector.scalar_tensor_tensor(bias_lo[:], sl_t, -1.0, lo_t, ALU.mult, ALU.mult)
         bias_hi = tile("bias_hi", [P, PACK], F32)
-        nc.gpsimd.tensor_tensor(bias_hi[:], neg_sl[:], hi_t[:], ALU.mult)
+        nc.vector.scalar_tensor_tensor(bias_hi[:], sl_t, -1.0, hi_t, ALU.mult, ALU.mult)
 
         a_rows = tile("a_rows", [P, PACK, S], F32)
         for t in range(PACK):

@@ -220,6 +220,8 @@ def tile_picked_twpqqxbebd_none_po_kernel(
                 else:
                     nc.vector.tensor_copy(h_rows[t][:, cols], h_bank[:])
 
+        warm = tile("warm", [P, 1], F32)
+        nc.scalar.activation(warm[:], a_far[:, PACK - 1, 0:1], ACT.Sigmoid)
         out_codes = tile("out_codes", [P, S], U32)
         out_rows = out_0.rearrange("(p t) n -> p t n", t=PACK)
         codes_dram = out_1[0].rearrange("p c r -> p (c r)").bitcast(I32)

from contextlib import ExitStack

import concourse.mybir as mybir

K, T, S, N, G, H = 512, 1024, 256, 512, 2048, 512
FLOPS = 2 * K * H * S * 2 + 2 * H * N * S

F32 = mybir.dt.float32
BF16 = mybir.dt.bfloat16
I32 = mybir.dt.int32
U32 = mybir.dt.uint32
U16 = mybir.dt.uint16
U8 = mybir.dt.uint8
FP8X4 = mybir.dt.float8_e4m3fn_x4
FP4X4 = mybir.dt.float4_e2m1fn_x4
ALU = mybir.AluOpType
ACT = mybir.ActivationFunctionType

P = 128
PACK = 4
HALF = S // 2
QUARTER = S // 4
LOWEST = -3.0e38


def tile_picked_twpqqxbebd_none_po_kernel(
    tc, x_words, x_scales, d_words, d_scales, tau, gn, w1_words, w1_scales, sl, lo, hi,
    offs, k1, two, k2, n1, n2, n3, out_0, out_1, out_2,
):
    nc = tc.nc
    with ExitStack() as ctx:
        sb = ctx.enter_context(tc.tile_pool(name="sb", bufs=1))
        ps = ctx.enter_context(tc.psum_pool(name="ps", bufs=1))

        def tile(name, shape, dtype, tag=""):
            return sb.tile(shape, dtype, name=name, tag=tag or name, align_bytes=64)

        def load_list(name, src):
            dst = sb.tile([P, src.shape[1]], U16, name=name)
            nc.sync.dma_start(dst[:], src)
            return dst

        def load_column(queue, name, src):
            dst = tile(name, [P, PACK], F32)
            queue.dma_start(dst[:], src.rearrange("(p t) o -> p (t o)", t=PACK))
            return dst

        def half_of(lst, u):
            return lst[:, u * (HALF // 16) : (u + 1) * (HALF // 16)]

        d_sc = tile("d_sc", [P, G], U8)
        x_sc = tile("x_sc", [P, T], U8)
        two_t = load_list("two_t", two)
        nc.sync.dma_start(x_sc[:].bitcast(I32), x_scales[0].bitcast(I32).unsqueeze(1).to_broadcast([16, 8, T // 4]))
        k2_t = load_list("k2_t", k2)
        nc.sync.dma_start(d_sc[:].bitcast(I32), d_scales[0].bitcast(I32).unsqueeze(1).to_broadcast([16, 8, G // 4]))
        d_w = tile("d_w", [P, G], U32)
        x_w = tile("x_w", [P, T], U32)
        offs_t = load_list("offs_t", offs)
        k1_t = load_list("k1_t", k1)
        n1_t = load_list("n1_t", n1)
        nc.sync.dma_start(d_w[:].bitcast(I32), d_words[0].rearrange("p c r -> p (c r)").bitcast(I32))
        n2_t = load_list("n2_t", n2)
        n3_t = load_list("n3_t", n3)
        nc.sync.dma_start(x_w[:].bitcast(I32), x_words[0].rearrange("p c r -> p (c r)").bitcast(I32))
        tau_t = load_column(nc.gpsimd, "tau_t", tau)

        moved = {}
        for name, width in (("b", H + S), ("ax", S), ("a", H)):
            moved[name] = tile("moved_" + name, [P, width], U8)
            nc.vector.memset(moved[name][:].bitcast(I32), 0)
        b_rows = [tile("b_row%d" % t, [P, 2 * S], F32) for t in range(PACK)]
        for b_row in b_rows:
            nc.vector.memset(b_row[:, S : 2 * S], 0.0)
        out_sc = tile("out_sc", [P, S], U8)
        z_sc = tile("z_sc", [P, S], U8)

        w_raw = tile("w_raw", [P, 2 * N], U8)
        nc.gpsimd.dma_start(w_raw[:].bitcast(I32), w1_words[0].bitcast(I32))

        neg_tau = tile("neg_tau", [P, PACK], F32)
        nc.scalar.activation(neg_tau[:], tau_t[:], ACT.Copy, scale=-1.0)

        def move_rows(name, picked_sc):
            for q in range(4):
                nc.sync.dma_start(
                    moved[name][:].bitcast(I32)[32 * q : 32 * q + 4, :],
                    picked_sc[:].bitcast(I32)[32 * q : 32 * q + 32 : 8, :],
                )

        def coded_product(name, k_t, x_t, x_plane, slots):
            picked_d = tile("picked_d_" + name, [P, H], U32, slots[1])
            nc.vector.tensor_copy(picked_d[:], d_w[:].indirect(k_t[:]))
            dealt_d = tile("dealt_d_" + name, [P, H], U32, slots[2])
            nc.vector.tensor_copy(
                dealt_d[:].bitcast(I32).rearrange("p (t m) -> p m t", t=PACK),
                picked_d[:].bitcast(I32).rearrange("p (m t) -> p m t", t=PACK),
            )
            picked_x = tile("picked_x_" + name, [P, S], U32, slots[3])
            nc.vector.tensor_copy(picked_x[:], x_w[:].indirect(x_t[:]))
            dealt_sc = tile("dealt_sc_" + name, [P, H], U8, slots[4])
            nc.vector.tensor_copy(
                dealt_sc[:].rearrange("p (t m) -> p m t", t=PACK),
                moved[name][:, 0:H].rearrange("p (m t) -> p m t", t=PACK),
            )
            banks = []
            for t in range(PACK):
                bank = ps.tile([P, S], F32, name="bank_%s%d" % (name, t), tag="bank_%s%d" % (name, t))
                nc.tensor.matmul_mx(
                    bank[:],
                    lhsT=dealt_d[:, t * P : (t + 1) * P].bitcast(FP8X4),
                    lhsT_scale=dealt_sc[:, t * P : (t + 1) * P],
                    rhs=picked_x[:].bitcast(FP8X4),
                    rhs_scale=x_plane,
                    start=True,
                    stop=True,
                )
                banks.append(bank)
            return banks

        picked_sc_b = tile("picked_sc_b", [P, H + S], U8, "s0")
        nc.vector.tensor_copy(picked_sc_b[:, H : H + S], x_sc[:].indirect(two_t[:]))
        nc.vector.tensor_copy(picked_sc_b[:, 0:H], d_sc[:].indirect(k2_t[:]))
        move_rows("b", picked_sc_b)
        picked_sc_ax = tile("picked_sc_ax", [P, S], U8)
        nc.vector.tensor_copy(picked_sc_ax[:], x_sc[:].indirect(offs_t[:]))
        move_rows("ax", picked_sc_ax)
        b_banks = coded_product("b", k2_t, two_t, moved["b"][:, H : H + S], ("s0", "s1", "s2", "s3", "s4"))
        w_sc_raw = tile("w_sc_raw", [P, N], U8, "s1")
        for q in range(4):
            rows = w1_scales[0].bitcast(I32)[4 * q : 4 * q + 4, :]
            nc.sync.dma_start(
                w_sc_raw[:].bitcast(I32)[32 * q : 32 * q + 32, :], rows.unsqueeze(0).to_broadcast([8, 4, N // 4])
            )
        late = tile("late", [P, 4, 2 * PACK], F32, "picked_sc_ax")
        for j, src in enumerate((gn, sl, lo, hi)):
            nc.sync.dma_start(late[:, j, 0:PACK], src.rearrange("(p t) o -> p (t o)", t=PACK))
        gn_t, sl_t, lo_t, hi_t = (late[:, j, 0:PACK] for j in range(4))
        picked_sc_a = tile("picked_sc_a", [P, H], U8, "s0")
        nc.vector.tensor_copy(picked_sc_a[:], d_sc[:].indirect(k1_t[:]))
        move_rows("a", picked_sc_a)
        ea = tile("ea", [P, PACK, S], F32)
        for t in range(PACK):
            b_row = b_rows[t]
            top = tile("top%d" % t, [P, 1], F32)
            nc.vector.tensor_scalar(b_row[:, 0:S], b_banks[t][:], 0.0625, LOWEST, ALU.mult, ALU.max, accum_out=top[:])
            exp_bias = tile("exp_bias%d" % t, [P, 1], F32)
            nc.scalar.activation(exp_bias[:], top[:], ACT.Copy, scale=neg_tau[:, t : t + 1])
            nc.scalar.activation(
                ea[:, t, :], b_row[:].indirect(n1_t[:]), ACT.Exp, bias=exp_bias[:], scale=tau_t[:, t : t + 1]
            )

        a_banks = coded_product("a", k1_t, offs_t, moved["ax"][:], ("s0", "top0", "s6", "top1", "s5"))
        w_sc = tile("w_sc", [P, N], U8, "s0")

        root = tile("root", [P, PACK * S], F32)
        nc.scalar.activation(root[:], ea[:].rearrange("p t n -> p (t n)"), ACT.Abs_reciprocal_sqrt, bias=0.25)
        inv = tile("inv", [P, PACK, S], F32)
        nc.scalar.activation(inv[:].rearrange("p t n -> p (t n)"), root[:], ACT.Square)

        w_dealt = tile("w_dealt", [P, 2 * N], U8)
        nc.scalar.copy(
            w_dealt[:].bitcast(U16).rearrange("p (t m) -> p m t", t=PACK),
            w_raw[:].bitcast(U16).rearrange("p (m t) -> p m t", t=PACK),
        )
        nc.vector.tensor_copy(
            w_sc[:].rearrange("p (t m) -> p m t", t=PACK), w_sc_raw[:].rearrange("p (m t) -> p m t", t=PACK)
        )
        bias_lo = tile("bias_lo", [P, PACK], F32)
        nc.vector.scalar_tensor_tensor(bias_lo[:], sl_t, -1.0, lo_t, ALU.mult, ALU.mult)
        bias_hi = tile("bias_hi", [P, PACK], F32)
        nc.vector.scalar_tensor_tensor(bias_hi[:], sl_t, -1.0, hi_t, ALU.mult, ALU.mult)

        a_rows = tile("a_rows", [P, PACK, S], F32)
        for t in range(PACK):
            nc.vector.tensor_scalar(a_rows[:, t, :], a_banks[t][:], gn_t[:, t : t + 1], 0.03125, ALU.mult, ALU.mult)

        z_codes = tile("z_codes", [P, S], U32)
        h_rows = [tile("h_row%d" % t, [P, S], F32) for t in range(PACK)]
        for u in range(2):
            cols = slice(u * HALF, (u + 1) * HALF)
            a_far = tile("a_far%d" % u, [P, PACK, HALF], F32, "root" if u else "")
            for t in range(PACK):
                looked_up = a_rows[:, t, :].indirect(half_of(n2_t, u))
                if u == 0:
                    nc.vector.tensor_copy(a_far[:, t, :], looked_up)
                else:
                    nc.scalar.activation(a_far[:, t, :], looked_up, ACT.Copy)
            diff = tile("diff%d" % u, [P, PACK, HALF], F32, "z_bf0" if u else "")
            z_bf = tile("z_bf%d" % u, [P, PACK * HALF], BF16)
            parts = [slice(v * QUARTER, (v + 1) * QUARTER) for v in range(2)]
            for part in parts:
                nc.vector.tensor_tensor(diff[:, :, part], a_rows[:, :, cols][:, :, part], a_far[:, :, part], ALU.subtract)
            for part in parts:
                nc.vector.tensor_tensor(
                    z_bf[:].rearrange("p (n t) -> p t n", t=PACK)[:, :, part].rearrange("p t (c i) -> p c t i", i=4),
                    diff[:, :, part].rearrange("p t (c i) -> p c t i", i=4),
                    inv[:, :, cols][:, :, part].rearrange("p t (c i) -> p c t i", i=4),
                    ALU.mult,
                )
            for part in parts:
                nc.vector.quantize_mx(
                    z_codes[:, cols][:, part].bitcast(FP8X4),
                    z_sc[:, cols][:, part],
                    z_bf[:, PACK * part.start : PACK * part.stop],
                )
            for t in range(PACK):
                h_bank = ps.tile([P, HALF], F32, name="bank_h%d%d" % (u, t), tag="bank_%s%d" % ("ba"[u], t))
                nc.tensor.matmul_mx(
                    h_bank[:],
                    lhsT=w_dealt[:, 2 * t * P : 2 * (t + 1) * P].bitcast(FP4X4),
                    lhsT_scale=w_sc[:, t * P : (t + 1) * P],
                    rhs=z_codes[:, cols].bitcast(FP8X4),
                    rhs_scale=z_sc[:, cols],
                    start=True,
                    stop=True,
                )
                if u == 0:
                    nc.scalar.copy(h_rows[t][:, cols], h_bank[:])
                else:
                    nc.vector.tensor_copy(h_rows[t][:, cols], h_bank[:])

        warm = tile("warm", [P, 1], F32)
        nc.scalar.activation(warm[:], a_far[:, PACK - 1, 0:1], ACT.Sigmoid)
        out_codes = tile("out_codes", [P, S], U32)
        out_rows = out_0.rearrange("(p t) n -> p t n", t=PACK)
        codes_dram = out_1[0].rearrange("p c r -> p (c r)").bitcast(I32)
        for u in range(2):
            cols = slice(u * HALF, (u + 1) * HALF)
            y = tile("y%d" % u, [P, PACK, HALF], F32)
            y_bf = tile("y_bf%d" % u, [P, PACK * HALF], BF16)
            for t in range(PACK):
                sg = tile("sg%d%d" % (u, t), [P, HALF], F32)
                sg2 = tile("sg2%d%d" % (u, t), [P, HALF], F32)
                for dst, bias in ((sg, bias_lo), (sg2, bias_hi)):
                    nc.scalar.activation(
                        dst[:], h_rows[t][:].indirect(half_of(n3_t, u)), ACT.Sigmoid,
                        bias=bias[:, t : t + 1], scale=sl_t[:, t : t + 1],
                    )
                band = tile("band%d%d" % (u, t), [P, HALF], F32)
                nc.vector.tensor_tensor(band[:], sg[:], sg2[:], ALU.subtract)
                nc.vector.tensor_tensor(y[:, t, :], h_rows[t][:, cols], band[:], ALU.mult)
                if t >= PACK - 2:
                    rows = slice(0, PACK - 1) if t == PACK - 2 else slice(PACK - 1, PACK)
                    nc.sync.dma_start(out_rows[:, rows, cols], y[:, rows, :])
                    nc.vector.tensor_copy(
                        y_bf[:].rearrange("p (c i t) -> p c t i", i=4, t=PACK)[:, :, rows, :],
                        y[:, rows, :].rearrange("p t (c i) -> p c t i", i=4),
                    )
            nc.vector.quantize_mx(out_codes[:, cols].bitcast(FP8X4), out_sc[:, cols], y_bf[:])
            nc.sync.dma_start(codes_dram[:, cols], out_codes[:, cols].bitcast(I32))
        for q in range(4):
            queue = nc.scalar if q % 2 == 0 else nc.sync
            queue.dma_start(out_2[0].bitcast(I32)[4 * q : 4 * q + 4, :], out_sc[:].bitcast(I32)[32 * q : 32 * q + 4, :])
